import numpy as np
import ml_dtypes

BF16 = ml_dtypes.bfloat16


def bf(x):
    return np.asarray(x, np.float32).astype(BF16)


def f32(x):
    return np.asarray(x, np.float32)


def f64(x):
    return np.asarray(x).astype(np.float64)


def striped(idx):
    return np.tile(idx.reshape(-1, 16).T, (8, 1))


S, K, M, N = 512, 128, 256, 512


def setup_inputs():
    return {"table": bf(np.random.standard_normal((K, S))), "w": bf(np.random.standard_normal((K, M)) / np.sqrt(K)), "r": f32(np.random.standard_normal((M, N))), "offs": striped(np.random.permutation(S))}


def reference(table, w, r, offs):
    idx = offs[:16].T.reshape(-1)
    x = f64(table)[:, idx]
    y = f64(w).T @ x
    return y + f64(r)

@@ -1,0 +1,45 @@
+import concourse.mybir as mybir
+
+P = 128
+S = 512
+M = 256
+N = 512
+FLOPS = 2 * P * M * N
+
+BF16, F32, U16 = mybir.dt.bfloat16, mybir.dt.float32, mybir.dt.uint16
+ADD = mybir.AluOpType.add
+
+
+def tile_gather_matmul_kernel(tc, table, w, r, offs, out):
+    nc = tc.nc
+    with (
+        tc.tile_pool(name="held", bufs=1) as held,
+        tc.psum_pool(name="banks", bufs=1) as banks,
+    ):
+        offsets = held.tile([P, N // 16], U16, name="offsets")
+        nc.sync.dma_start(offsets[:], offs)
+        tokens = held.tile([P, S], BF16, name="tokens")
+        nc.scalar.dma_start(tokens[:], table)
+        weights = held.tile([P, M], BF16, name="weights")
+        nc.sync.dma_start(weights[:], w)
+
+        blocks = range(M // P)
+        queues = (nc.scalar, nc.sync)
+        residuals = []
+        for b in blocks:
+            residual = held.tile([P, N], F32, name=f"residual{b}")
+            queues[b].dma_start(residual[:], r[b * P : (b + 1) * P, :])
+            residuals.append(residual)
+
+        for b in blocks:
+            product = banks.tile([P, N], F32, name=f"product{b}")
+            nc.tensor.matmul(
+                product[:],
+                weights[:, b * P : (b + 1) * P],
+                tokens[:].indirect(offsets[:]),
+                start=True,
+                stop=True,
+            )
+            result = held.tile([P, N], F32, name=f"result{b}")
+            nc.vector.tensor_tensor(result[:], product[:], residuals[b][:], ADD)
+            queues[b].dma_start(out[b * P : (b + 1) * P, :], result[:])

@@ -9,6 +9,8 @@ FLOPS = 2 * P * M * N
 BF16, F32, U16 = mybir.dt.bfloat16, mybir.dt.float32, mybir.dt.uint16
 ADD = mybir.AluOpType.add
 
+PIECE = 256
+
 
 def tile_gather_matmul_kernel(tc, table, w, r, offs, out):
     nc = tc.nc
@@ -32,14 +34,16 @@ def tile_gather_matmul_kernel(tc, table, w, r, offs, out):
             residuals.append(residual)
 
         for b in blocks:
-            product = banks.tile([P, N], F32, name=f"product{b}")
-            nc.tensor.matmul(
-                product[:],
-                weights[:, b * P : (b + 1) * P],
-                tokens[:].indirect(offsets[:]),
-                start=True,
-                stop=True,
-            )
-            result = held.tile([P, N], F32, name=f"result{b}")
-            nc.vector.tensor_tensor(result[:], product[:], residuals[b][:], ADD)
-            queues[b].dma_start(out[b * P : (b + 1) * P, :], result[:])
+            for h in range(N // PIECE):
+                columns = slice(h * PIECE, (h + 1) * PIECE)
+                product = banks.tile([P, PIECE], F32, name=f"product{b}{h}")
+                nc.tensor.matmul(
+                    product[:],
+                    weights[:, b * P : (b + 1) * P],
+                    tokens[:].indirect(offsets[:, h * PIECE // 16 : (h + 1) * PIECE // 16]),
+                    start=True,
+                    stop=True,
+                )
+                result = held.tile([P, PIECE], F32, name=f"result{b}{h}")
+                nc.vector.tensor_tensor(result[:], product[:], residuals[b][:, columns], ADD)
+                queues[h].dma_start(out[b * P : (b + 1) * P, columns], result[:])

@@ -9,7 +9,7 @@ FLOPS = 2 * P * M * N
 BF16, F32, U16 = mybir.dt.bfloat16, mybir.dt.float32, mybir.dt.uint16
 ADD = mybir.AluOpType.add
 
-PIECE = 256
+WARM_UPS = 4
 
 
 def tile_gather_matmul_kernel(tc, table, w, r, offs, out):
@@ -33,17 +33,21 @@ def tile_gather_matmul_kernel(tc, table, w, r, offs, out):
             queues[b].dma_start(residual[:], r[b * P : (b + 1) * P, :])
             residuals.append(residual)
 
+        zeros = held.tile([P, N], BF16, name="zeros")
+        nc.vector.memset(zeros[:], 0.0)
+        unread = banks.tile([P, N], F32, name="unread")
+        for i in range(WARM_UPS):
+            nc.tensor.matmul(unread[:], zeros[:, 0:P], zeros[:], start=True, stop=True)
+
         for b in blocks:
-            for h in range(N // PIECE):
-                columns = slice(h * PIECE, (h + 1) * PIECE)
-                product = banks.tile([P, PIECE], F32, name=f"product{b}{h}")
-                nc.tensor.matmul(
-                    product[:],
-                    weights[:, b * P : (b + 1) * P],
-                    tokens[:].indirect(offsets[:, h * PIECE // 16 : (h + 1) * PIECE // 16]),
-                    start=True,
-                    stop=True,
-                )
-                result = held.tile([P, PIECE], F32, name=f"result{b}{h}")
-                nc.vector.tensor_tensor(result[:], product[:], residuals[b][:, columns], ADD)
-                queues[h].dma_start(out[b * P : (b + 1) * P, columns], result[:])
+            product = banks.tile([P, N], F32, name=f"product{b}")
+            nc.tensor.matmul(
+                product[:],
+                weights[:, b * P : (b + 1) * P],
+                tokens[:].indirect(offsets[:]),
+                start=True,
+                stop=True,
+            )
+            result = held.tile([P, N], F32, name=f"result{b}")
+            nc.vector.tensor_tensor(result[:], product[:], residuals[b][:], ADD)
+            queues[b].dma_start(out[b * P : (b + 1) * P, :], result[:])

@@ -9,7 +9,7 @@ FLOPS = 2 * P * M * N
 BF16, F32, U16 = mybir.dt.bfloat16, mybir.dt.float32, mybir.dt.uint16
 ADD = mybir.AluOpType.add
 
-WARM_UPS = 4
+HALF = N // 2
 
 
 def tile_gather_matmul_kernel(tc, table, w, r, offs, out):
@@ -33,21 +33,17 @@ def tile_gather_matmul_kernel(tc, table, w, r, offs, out):
             queues[b].dma_start(residual[:], r[b * P : (b + 1) * P, :])
             residuals.append(residual)
 
-        zeros = held.tile([P, N], BF16, name="zeros")
-        nc.vector.memset(zeros[:], 0.0)
-        unread = banks.tile([P, N], F32, name="unread")
-        for i in range(WARM_UPS):
-            nc.tensor.matmul(unread[:], zeros[:, 0:P], zeros[:], start=True, stop=True)
-
-        for b in blocks:
-            product = banks.tile([P, N], F32, name=f"product{b}")
+        pieces = ((0, 0, N), (1, 0, HALF), (1, HALF, N))
+        for i, (b, first, last) in enumerate(pieces):
+            width = last - first
+            product = banks.tile([P, width], F32, name=f"product{i}")
             nc.tensor.matmul(
                 product[:],
                 weights[:, b * P : (b + 1) * P],
-                tokens[:].indirect(offsets[:]),
+                tokens[:].indirect(offsets[:, first // 16 : last // 16]),
                 start=True,
                 stop=True,
             )
-            result = held.tile([P, N], F32, name=f"result{b}")
-            nc.vector.tensor_tensor(result[:], product[:], residuals[b][:], ADD)
-            queues[b].dma_start(out[b * P : (b + 1) * P, :], result[:])
+            result = held.tile([P, width], F32, name=f"result{i}")
+            nc.vector.tensor_tensor(result[:], product[:], residuals[b][:, first:last], ADD)
+            queues[i % 2].dma_start(out[b * P : (b + 1) * P, first:last], result[:])

@@ -18,12 +18,12 @@ def tile_gather_matmul_kernel(tc, table, w, r, offs, out):
         tc.tile_pool(name="held", bufs=1) as held,
         tc.psum_pool(name="banks", bufs=1) as banks,
     ):
+        tokens = held.tile([P, S], BF16, name="tokens")
+        nc.sync.dma_start(tokens[:], table)
+        weights = held.tile([P, M], BF16, name="weights")
+        nc.scalar.dma_start(weights[:], w)
         offsets = held.tile([P, N // 16], U16, name="offsets")
         nc.sync.dma_start(offsets[:], offs)
-        tokens = held.tile([P, S], BF16, name="tokens")
-        nc.scalar.dma_start(tokens[:], table)
-        weights = held.tile([P, M], BF16, name="weights")
-        nc.sync.dma_start(weights[:], w)
 
         blocks = range(M // P)
         queues = (nc.scalar, nc.sync)

@@ -26,11 +26,10 @@ def tile_gather_matmul_kernel(tc, table, w, r, offs, out):
         nc.sync.dma_start(offsets[:], offs)
 
         blocks = range(M // P)
-        queues = (nc.scalar, nc.sync)
         residuals = []
         for b in blocks:
             residual = held.tile([P, N], F32, name=f"residual{b}")
-            queues[b].dma_start(residual[:], r[b * P : (b + 1) * P, :])
+            nc.scalar.dma_start(residual[:], r[b * P : (b + 1) * P, :])
             residuals.append(residual)
 
         pieces = ((0, 0, N), (1, 0, HALF), (1, HALF, N))
@@ -46,4 +45,5 @@ def tile_gather_matmul_kernel(tc, table, w, r, offs, out):
             )
             result = held.tile([P, width], F32, name=f"result{i}")
             nc.vector.tensor_tensor(result[:], product[:], residuals[b][:, first:last], ADD)
-            queues[i % 2].dma_start(out[b * P : (b + 1) * P, first:last], result[:])
+            store_queue = nc.scalar if i == len(pieces) - 1 else nc.sync
+            store_queue.dma_start(out[b * P : (b + 1) * P, first:last], result[:])

@@ -32,18 +32,23 @@ def tile_gather_matmul_kernel(tc, table, w, r, offs, out):
             nc.scalar.dma_start(residual[:], r[b * P : (b + 1) * P, :])
             residuals.append(residual)
 
-        pieces = ((0, 0, N), (1, 0, HALF), (1, HALF, N))
-        for i, (b, first, last) in enumerate(pieces):
-            width = last - first
-            product = banks.tile([P, width], F32, name=f"product{i}")
-            nc.tensor.matmul(
-                product[:],
-                weights[:, b * P : (b + 1) * P],
-                tokens[:].indirect(offsets[:, first // 16 : last // 16]),
-                start=True,
-                stop=True,
-            )
-            result = held.tile([P, width], F32, name=f"result{i}")
-            nc.vector.tensor_tensor(result[:], product[:], residuals[b][:, first:last], ADD)
-            store_queue = nc.scalar if i == len(pieces) - 1 else nc.sync
-            store_queue.dma_start(out[b * P : (b + 1) * P, first:last], result[:])
+        last_block = M // P - 1
+        for b in blocks:
+            result = held.tile([P, N], F32, name=f"result{b}")
+            rows = slice(b * P, (b + 1) * P)
+            for first in (0, HALF):
+                half = slice(first, first + HALF)
+                product = banks.tile([P, HALF], F32, name=f"product{b}_{first}")
+                nc.tensor.matmul(
+                    product[:],
+                    weights[:, rows],
+                    tokens[:].indirect(offsets[:, first // 16 : (first + HALF) // 16]),
+                    start=True,
+                    stop=True,
+                )
+                nc.vector.tensor_tensor(result[:, half], product[:], residuals[b][:, half], ADD)
+                if b == last_block:
+                    store_queue = nc.sync if first == 0 else nc.scalar
+                    store_queue.dma_start(out[rows, half], result[:, half])
+            if b != last_block:
+                nc.sync.dma_start(out[rows, :], result[:])

@@ -18,18 +18,17 @@ def tile_gather_matmul_kernel(tc, table, w, r, offs, out):
         tc.tile_pool(name="held", bufs=1) as held,
         tc.psum_pool(name="banks", bufs=1) as banks,
     ):
+        weights = held.tile([P, M], BF16, name="weights")
+        nc.sync.dma_start(weights[:], w)
         tokens = held.tile([P, S], BF16, name="tokens")
         nc.sync.dma_start(tokens[:], table)
-        weights = held.tile([P, M], BF16, name="weights")
-        nc.scalar.dma_start(weights[:], w)
         offsets = held.tile([P, N // 16], U16, name="offsets")
         nc.sync.dma_start(offsets[:], offs)
-
         blocks = range(M // P)
         residuals = []
         for b in blocks:
             residual = held.tile([P, N], F32, name=f"residual{b}")
-            nc.scalar.dma_start(residual[:], r[b * P : (b + 1) * P, :])
+            nc.sync.dma_start(residual[:], r[b * P : (b + 1) * P, :])
             residuals.append(residual)
 
         last_block = M // P - 1
@@ -51,4 +50,4 @@ def tile_gather_matmul_kernel(tc, table, w, r, offs, out):
                     store_queue = nc.sync if first == 0 else nc.scalar
                     store_queue.dma_start(out[rows, half], result[:, half])
             if b != last_block:
-                nc.sync.dma_start(out[rows, :], result[:])
+                nc.scalar.dma_start(out[rows, :], result[:])

@@ -25,29 +25,23 @@ def tile_gather_matmul_kernel(tc, table, w, r, offs, out):
         offsets = held.tile([P, N // 16], U16, name="offsets")
         nc.sync.dma_start(offsets[:], offs)
         blocks = range(M // P)
-        residuals = []
+        halves = (slice(0, HALF), slice(HALF, N))
+        residuals = [held.tile([P, N], F32, name=f"residual{b}") for b in blocks]
         for b in blocks:
-            residual = held.tile([P, N], F32, name=f"residual{b}")
-            nc.sync.dma_start(residual[:], r[b * P : (b + 1) * P, :])
-            residuals.append(residual)
+            for part in halves if b == 0 else (slice(0, N),):
+                nc.sync.dma_start(residuals[b][:, part], r[b * P : (b + 1) * P, part])
 
-        last_block = M // P - 1
         for b in blocks:
             result = held.tile([P, N], F32, name=f"result{b}")
             rows = slice(b * P, (b + 1) * P)
-            for first in (0, HALF):
-                half = slice(first, first + HALF)
-                product = banks.tile([P, HALF], F32, name=f"product{b}_{first}")
+            for half in halves:
+                product = banks.tile([P, HALF], F32, name=f"product{b}_{half.start}")
                 nc.tensor.matmul(
                     product[:],
                     weights[:, rows],
-                    tokens[:].indirect(offsets[:, first // 16 : (first + HALF) // 16]),
+                    tokens[:].indirect(offsets[:, half.start // 16 : half.stop // 16]),
                     start=True,
                     stop=True,
                 )
                 nc.vector.tensor_tensor(result[:, half], product[:], residuals[b][:, half], ADD)
-                if b == last_block:
-                    store_queue = nc.sync if first == 0 else nc.scalar
-                    store_queue.dma_start(out[rows, half], result[:, half])
-            if b != last_block:
-                nc.scalar.dma_start(out[rows, :], result[:])
+            nc.scalar.dma_start(out[rows, :], result[:])

@@ -10,6 +10,7 @@ BF16, F32, U16 = mybir.dt.bfloat16, mybir.dt.float32, mybir.dt.uint16
 ADD = mybir.AluOpType.add
 
 HALF = N // 2
+LONG = 3 * N // 4
 
 
 def tile_gather_matmul_kernel(tc, table, w, r, offs, out):
@@ -31,17 +32,18 @@ def tile_gather_matmul_kernel(tc, table, w, r, offs, out):
             for part in halves if b == 0 else (slice(0, N),):
                 nc.sync.dma_start(residuals[b][:, part], r[b * P : (b + 1) * P, part])
 
+        cuts = (halves, (slice(0, LONG), slice(LONG, N)))
         for b in blocks:
             result = held.tile([P, N], F32, name=f"result{b}")
             rows = slice(b * P, (b + 1) * P)
-            for half in halves:
-                product = banks.tile([P, HALF], F32, name=f"product{b}_{half.start}")
+            for part in cuts[b]:
+                product = banks.tile([P, part.stop - part.start], F32, name=f"product{b}_{part.start}")
                 nc.tensor.matmul(
                     product[:],
                     weights[:, rows],
-                    tokens[:].indirect(offsets[:, half.start // 16 : half.stop // 16]),
+                    tokens[:].indirect(offsets[:, part.start // 16 : part.stop // 16]),
                     start=True,
                     stop=True,
                 )
-                nc.vector.tensor_tensor(result[:, half], product[:], residuals[b][:, half], ADD)
+                nc.vector.tensor_tensor(result[:, part], product[:], residuals[b][:, part], ADD)
             nc.scalar.dma_start(out[rows, :], result[:])

@@ -19,10 +19,10 @@ def tile_gather_matmul_kernel(tc, table, w, r, offs, out):
         tc.tile_pool(name="held", bufs=1) as held,
         tc.psum_pool(name="banks", bufs=1) as banks,
     ):
-        weights = held.tile([P, M], BF16, name="weights")
-        nc.sync.dma_start(weights[:], w)
         tokens = held.tile([P, S], BF16, name="tokens")
         nc.sync.dma_start(tokens[:], table)
+        weights = held.tile([P, M], BF16, name="weights")
+        nc.scalar.dma_start(weights[:], w)
         offsets = held.tile([P, N // 16], U16, name="offsets")
         nc.sync.dma_start(offsets[:], offs)
         blocks = range(M // P)
@@ -30,7 +30,7 @@ def tile_gather_matmul_kernel(tc, table, w, r, offs, out):
         residuals = [held.tile([P, N], F32, name=f"residual{b}") for b in blocks]
         for b in blocks:
             for part in halves if b == 0 else (slice(0, N),):
-                nc.sync.dma_start(residuals[b][:, part], r[b * P : (b + 1) * P, part])
+                nc.scalar.dma_start(residuals[b][:, part], r[b * P : (b + 1) * P, part])
 
         cuts = (halves, (slice(0, LONG), slice(LONG, N)))
         for b in blocks:
@@ -46,4 +46,4 @@ def tile_gather_matmul_kernel(tc, table, w, r, offs, out):
                     stop=True,
                 )
                 nc.vector.tensor_tensor(result[:, part], product[:], residuals[b][:, part], ADD)
-            nc.scalar.dma_start(out[rows, :], result[:])
+            nc.sync.dma_start(out[rows, :], result[:])

@@ -20,9 +20,9 @@ def tile_gather_matmul_kernel(tc, table, w, r, offs, out):
         tc.psum_pool(name="banks", bufs=1) as banks,
     ):
         tokens = held.tile([P, S], BF16, name="tokens")
-        nc.sync.dma_start(tokens[:], table)
+        nc.scalar.dma_start(tokens[:], table)
         weights = held.tile([P, M], BF16, name="weights")
-        nc.scalar.dma_start(weights[:], w)
+        nc.sync.dma_start(weights[:], w)
         offsets = held.tile([P, N // 16], U16, name="offsets")
         nc.sync.dma_start(offsets[:], offs)
         blocks = range(M // P)

import concourse.mybir as mybir

P = 128
S = 512
M = 256
N = 512
FLOPS = 2 * P * M * N

BF16, F32, U16 = mybir.dt.bfloat16, mybir.dt.float32, mybir.dt.uint16
ADD = mybir.AluOpType.add

HALF = N // 2
LONG = 3 * N // 4


def tile_gather_matmul_kernel(tc, table, w, r, offs, out):
    nc = tc.nc
    with (
        tc.tile_pool(name="held", bufs=1) as held,
        tc.psum_pool(name="banks", bufs=1) as banks,
    ):
        tokens = held.tile([P, S], BF16, name="tokens")
        nc.scalar.dma_start(tokens[:], table)
        weights = held.tile([P, M], BF16, name="weights")
        nc.sync.dma_start(weights[:], w)
        offsets = held.tile([P, N // 16], U16, name="offsets")
        nc.sync.dma_start(offsets[:], offs)
        blocks = range(M // P)
        halves = (slice(0, HALF), slice(HALF, N))
        residuals = [held.tile([P, N], F32, name=f"residual{b}") for b in blocks]
        for b in blocks:
            for part in halves if b == 0 else (slice(0, N),):
                nc.scalar.dma_start(residuals[b][:, part], r[b * P : (b + 1) * P, part])

        cuts = (halves, (slice(0, LONG), slice(LONG, N)))
        for b in blocks:
            result = held.tile([P, N], F32, name=f"result{b}")
            rows = slice(b * P, (b + 1) * P)
            for part in cuts[b]:
                product = banks.tile([P, part.stop - part.start], F32, name=f"product{b}_{part.start}")
                nc.tensor.matmul(
                    product[:],
                    weights[:, rows],
                    tokens[:].indirect(offsets[:, part.start // 16 : part.stop // 16]),
                    start=True,
                    stop=True,
                )
                nc.vector.tensor_tensor(result[:, part], product[:], residuals[b][:, part], ADD)
            nc.sync.dma_start(out[rows, :], result[:])
